import numpy as np, ml_dtypes
CORES = [1,5,17,21,33,37,49,53]
N = 8
BF = ml_dtypes.bfloat16
W, C, S, RO, B = 4096, 128, 3, 3, 32
def parts(rng):
    x = rng.integers(122, 135, (N, 8, 16, W), dtype=np.int16)
    far = rng.random((N, 8, 16, W), dtype=np.float32) < rng.choice(np.array([0.02, 0.06, 0.1]), (N, 8, 16, 1))
    far = far | (rng.random((N, 8, 1, W)) < 0.02)
    x = np.where(far, rng.integers(0, 256, (N, 8, 16, W), dtype=np.int16), x)
    return x, rng.integers(0, W, (N, 8, 16, C)), rng.integers(0, 4096, (N, 8, 16, 1)), rng.integers(-160, 161, (N, 8, RO, S, C))
def pack(x, c, w, sl):
    return {"xt": np.ascontiguousarray(np.reshape(x, (N, 128, W))).astype(np.float32).astype(BF), "ch": np.ascontiguousarray(np.reshape(c, (N, 128, C))).astype(np.int32),
            "wt": np.ascontiguousarray(np.reshape(w, (N, 128, 1))).astype(np.int32), "sl": np.ascontiguousarray(np.reshape(sl, (N, 8, RO * S * C))).astype(np.int32)}
def setup_inputs(rng):
    return pack(*parts(rng))
def setup_inputs_spread(rng):
    x = np.minimum((np.exp2(8 * rng.random((N, 8, 1, W))) * rng.random((N, 8, 16, W), dtype=np.float32)).astype(np.int16), 255)
    x = np.where(rng.random((N, 8, 16, 1)) < 0.4, 255 - x, x)
    c = np.minimum((W * rng.random((N, 8, 16, C)) ** rng.choice(np.array([0.25, 1.0, 3.0]), (N, 8, 1, C))).astype(np.int64), W - 1)
    w = np.minimum(np.exp2(12 * rng.random((N, 8, 16, 1))).astype(np.int64) - 1, 4095)
    return pack(x, c, w, rng.integers(-255, 256, (N, 8, RO, S, C)))
def setup_inputs_ends(rng):
    b = np.zeros((N, 8, 16, W), bool); sh = int(rng.integers(0, 4))
    for r in range(N):
        for g in range(8):
            md = 4 if g == 7 else (g + r + sh) % 4
            if md == 0: b[r, g] = rng.random((1, W)) < 0.042
            elif md == 1: b[r, g] = rng.random((16, W)) < rng.choice(np.array([0.042, 0.5, 0.958]), (16, 1))
            elif md == 2: b[r, g] = rng.random((1, W)) < 0.958
            elif md == 3: b[r, g] = rng.random((16, W)) < 0.042
            else:
                b[r, g] = rng.random((1, W)) < 0.042; b[r, g, 15] = rng.random(W) < 0.042
    b[:, 7, :, 0] = False; b[:, 7, :, W - 1] = True
    c = np.where(rng.random((N, 8, 16, C)) < rng.choice(np.array([0.0, 0.0625, 0.5, 0.5, 0.9375, 1.0]), (N, 8, 1, C)), W - 1, 0)
    c[:, :, :, 0] = 0; c[:, 7, :, C - 2] = W - 1
    k = np.arange(16); nm = np.where(k % 2 == 0, W - 1, 0); nx = (((nm * 16) >> 6) + nm + 613 * k) & (W - 1)
    c[:, 7, :, C - 1] = nm
    last, first = b[N - 1, 7], b[0, 7]
    last[:, nx] = False; last[:15, nx[0]] = True; last[15, nx] = True
    first[:, nx] = False; first[:, nx[0]] = True
    w = 4095 * rng.integers(0, 2, (N, 8, 16, 1)); w[:, 1, 0] = 0; w[:, 1, 1] = 4095; w[0, 0] = 0; w[N - 1, 7] = 4095
    sl = 510 * rng.integers(0, 2, (N, 8, RO, S, C)) - 255; sl[N - 1, 7, 0, 0, C - 1] = -255
    return pack(255 * b.astype(np.int16), c, w, sl)
def setup_inputs_corners(rng):
    x, c, w, sl = parts(rng); i = np.arange(C)
    x[1, 0] = 255 * rng.integers(0, 2, (16, W))
    pin = 5 * C + int(rng.integers(0, C)) if W == 4096 else -1
    for a, m in ((0, int(rng.choice(np.array([31, 32, 33, 8 * C - 1])))), (2, 8 * C)):
        x[a] = rng.integers(0, 256, (8, 16, 1)); x[a, 7, 15] = 255; x[a, 7, 14] = 0
        ways = np.stack([np.zeros((8, C), np.int64), np.full((8, C), W - 1), np.tile(B * i, (8, 1)), np.tile(B * i + B - 1, (8, 1)), rng.integers(0, W, (8, C))])
        c[a] = np.take_along_axis(ways, rng.integers(0, 5, (1, 8, C)), 0).reshape(8, 1, C)
        o = rng.permutation(8 * C)
        if a == 0: o = o[o != pin]
        h = np.zeros(8 * C, bool); h[o[:m]] = True
        sl[a, :, 0] = -255; sl[a, :, 0, 0] = np.where(h.reshape(8, C), 0, -255)
    if N > 4: x[4, :4] = rng.integers(0, 256, (4, 16, 1))
    c[1, 5] = 0; c[1, 6] = W - 1
    for a in (1, 3):
        sl[a] = rng.choice(np.array([-255, -1, 0, 1, 255]), (8, RO, S, C))
        c[a, :5] = np.where(rng.random((5, 1, C)) < 0.5, B * i + (B - 1) * rng.integers(0, 2, (5, 16, C)), c[a, :5])
    w[:, 1] = 0; w[:, 2] = 4095; w[:, 3, :15] = 0; w[:, 3, 15] = 4095; w[:, 4] = 1
    for g, low in ((0, 0), (6, 4095)):
        v = rng.integers(220, 256, 16); v[14] = 2; v[15] = 1
        z = rng.integers(3500, 4096, 16); z[14] = rng.integers(0, 2048); z[15] = 0
        z[15] = (low - int(np.sum(v * z))) & 4095
        if (int(np.sum(v * z)) >> 12) & 1 == 0: z[14] += 2048
        x[0, g] = v.reshape(16, 1); w[0, g] = z.reshape(16, 1)
    if pin >= 0:
        p = int(rng.integers(0, 16)); x[0, 5, p] = 1; w[0, 5] = 0; w[0, 5, p] = 4075
        first = (((c[0, 5] * 4075) >> 6) + c[0, 5]) & (W - 1)
        c[0, 5] = np.where(first == 2557, 0, c[0, 5]); c[0, 5, :, pin - 5 * C] = 4093; sl[0, 5, 0, 0, pin - 5 * C] = 0
        nx = (2557 + 613 * np.arange(16)) & (W - 1); own = x[1, 5]; own[:, nx] = rng.integers(122, 135, (16, 1))
    return pack(x, c, w, sl)
def setup_inputs_ties(rng):
    x = rng.integers(0, 254, (N, 8, 16, 1), dtype=np.int16) + 2 * (rng.random((N, 8, 16, W), dtype=np.float32) < rng.choice(np.array([0.02, 0.05]), (N, 8, 16, 1))).astype(np.int16)
    c = rng.integers(0, W, (N, 8, 16, C)); few = np.take_along_axis(c, rng.integers(0, 4, (N, 8, 16, C)), 2)
    c = np.where(rng.random((N, 8, 1, C)) < 0.5, few, c); sl = rng.integers(-3, 4, (N, 8, RO, S, C))
    x[0] = rng.integers(0, 256, (8, 16, 1)); x[2, :2] = rng.integers(0, 256, (2, 16, 1)); c[0] = rng.integers(0, W, (8, 1, C))
    x[1, :, 15] = rng.integers(0, 254, (8, 1)) + 2 * (np.arange(W) & 1)
    h = np.zeros(8 * C, bool); h[rng.permutation(8 * C)[:26 + 2 * int(rng.integers(0, 3)) + 32 * int(rng.integers(0, C // 4))]] = True
    sl[0, :, 0] = -1; sl[0, :, 0, 0] = np.where(h.reshape(8, C), 0, -1)
    return pack(x, c, rng.integers(0, 4096, (N, 8, 16, 1)), sl)
def check_inputs(d):
    bad = []
    for k, lo, hi in (("xt", 0, 255), ("ch", 0, W - 1), ("wt", 0, 4095), ("sl", -255, 255)):
        v = np.asarray(d[k]).astype(np.float64)
        if not (np.min(v) >= lo and np.max(v) <= hi): bad.append("range of " + k)
        if not np.all(v == np.floor(v)): bad.append("whole numbers in " + k)
    return bad
def look(tab, c):
    v = np.take_along_axis(tab, c.reshape(8, 1, 16 * C), 2).reshape(8, 16, 16, C)
    y = np.max(v, axis=2).astype(np.int64); m = np.min(v, axis=2).astype(np.int64)
    return y, np.add.reduce(y - m, axis=1)
def reference(xt, ch, wt, sl):
    X = xt.astype(np.float32).astype(np.int32).reshape(N, 8, 16, W); c = ch.astype(np.int64).reshape(N, 8, 16, C)
    w = wt.astype(np.int64).reshape(N, 8, 16, 1); slack = sl.astype(np.int64).reshape(N, 8, RO, S, C)
    kappa = np.zeros(N, np.int64); k613 = (613 * np.arange(16)).reshape(1, 16, 1)
    for t in range(RO):
        states, tops, wrong = [], [], []
        for r in range(N):
            q = (r + 1 + t % (N - 1)) % N
            s = c[r]; y, e = look(X[r], s); eq = look(X[q], s)[1]
            fs, fy = s, y; right = np.ones((8, C), bool)
            for j in range(S):
                u = np.add.reduce(w[r] * y, axis=1) & 4095
                n = (((s * u[:, None, :]) >> 6) + s + k613 + 77 * j + kappa[r]) & (W - 1)
                yn, en = look(X[r], n); qn = look(X[q], n)[1]; a = slack[r, :, t, j]
                guess = en <= e + a; true = en + qn <= e + eq + a
                go = (right & true)[:, None, :]; fs = np.where(go, n, fs); fy = np.where(go, yn, fy)
                right = right & (guess == true)
                on = guess[:, None, :]; s = np.where(on, n, s); y = np.where(on, yn, y); e = np.where(guess, en, e); eq = np.where(guess, qn, eq)
            states.append(fs); tops.append(fy); wrong.append(np.count_nonzero(~right) & 31)
        for r in range(N):
            place = (B * np.arange(C)[None, :] + (np.add.reduce(w[r] * tops[r], axis=1) & (B - 1)))[:, None, :]
            old = np.take_along_axis(X[r], place, 2)
            np.put_along_axis(X[r], place, ((old + tops[r]) >> 1).astype(np.int32), 2)
        c = np.stack(states); kappa = np.array(wrong, np.int64)
    return {"yc": c.reshape(N, 128, C).astype(np.float32), "yx": X.reshape(N, 128, W).astype(np.float32).astype(BF)}

from concourse.mybir import AluOpType, AxisListType, ActivationFunctionType

RO, NL = 3, 4
SCRATCH = {
    "tab": ("sbuf", [128, 4096], "bfloat16"),
    "nW": ("sbuf", [128, 512], "int32"),
    "L": ("sbuf", [128, RO * NL * 128], "uint16"),
    "Lr": ("sbuf", [128, RO * NL * 128], "uint16"),
    "gA0": ("sbuf", [128, 2048], "bfloat16"),
    "gA1": ("sbuf", [128, 2048], "bfloat16"),
    "gS0": ("sbuf", [128, 2048], "bfloat16"),
    "gS1": ("sbuf", [128, 2048], "bfloat16"),
    "Y": ("sbuf", [128, 8192], "bfloat16"),
    "Mn": ("sbuf", [128, 8192], "bfloat16"),
    "YS": ("sbuf", [128, 2048], "bfloat16"),
    "MS": ("sbuf", [128, 2048], "bfloat16"),
    "Er": ("sbuf", [128, RO * NL * 8], "float32"),
    "Eq": ("sbuf", [128, RO * NL * 8], "float32"),
    "mx": ("sbuf", [128, 2048], "bfloat16"),
    "mn": ("sbuf", [128, 2048], "bfloat16"),
    "kp1": ("sbuf", [128, 128], "float32"),
    "kp2": ("sbuf", [128, 128], "float32"),
    "BK1": ("sbuf", [128, 128], "float32"),
    "BKb": ("sbuf", [128, 128], "bfloat16"),
    "Bp": ("sbuf", [128, 128], "bfloat16"),
    "Bn": ("sbuf", [128, 128], "bfloat16"),
    "Wh": ("sbuf", [128, 128], "bfloat16"),
    "Wl": ("sbuf", [128, 128], "bfloat16"),
    "ones": ("sbuf", [128, 128], "bfloat16"),
    "Bk": ("sbuf", [128, 2048], "bfloat16"),
    "Bnk": ("sbuf", [128, 2048], "bfloat16"),
    "Wk": ("sbuf", [128, 2048], "bfloat16"),
    "slz": ("sbuf", [128, 1152], "int32"),
    "slb": ("sbuf", [128, 1152], "bfloat16"),
    "a8": ("sbuf", [128, 144], "float32"),
    "wI": ("sbuf", [128, 1], "int32"),
    "wq": ("sbuf", [128, 4], "int32"),
    "wf": ("sbuf", [128, 4], "float32"),
    "kI": ("sbuf", [128, 4], "int32"),
    "kf": ("sbuf", [128, 8], "float32"),
    "cKi": ("sbuf", [128, 32], "int32"),
    "cK": ("sbuf", [128, 32], "float32"),
    "Ui": ("sbuf", [128, 128], "int32"),
    "ua": ("sbuf", [128, 128], "int32"),
    "P": ("sbuf", [128, 128], "float32"),
    "P3": ("sbuf", [128, 128], "float32"),
    "Qi": ("sbuf", [128, 128], "int32"),
    "h": ("sbuf", [128, 128], "float32"),
    "hd": ("sbuf", [128, 128], "float32"),
    "thr": ("sbuf", [128, 128], "float32"),
    "cat": ("sbuf", [128, 96], "float32"),
    "dl": ("sbuf", [128, 64], "float32"),
    "HD": ("sbuf", [128, 48], "float32"),
    "rt": ("sbuf", [128, 64], "float32"),
    "K": ("sbuf", [128, 32], "float32"),
    "Ki": ("sbuf", [128, 64], "int32"),
    "ci": ("sbuf", [128, 64], "int32"),
    "cf": ("sbuf", [128, 64], "float32"),
    "r3": ("sbuf", [128, 8], "bfloat16"),
    "o1": ("sbuf", [128, 8], "uint16"),
    "o2": ("sbuf", [128, 8], "uint16"),
    "o3": ("sbuf", [128, 8], "uint16"),
    "old": ("sbuf", [128, 128], "float32"),
    "sm": ("sbuf", [128, 128], "int32"),
    "sn": ("sbuf", [128, 128], "int32"),
    "fin": ("sbuf", [128, 128], "float32"),
    "pU": ("psum", [128, 512], "float32"),
    "pE": ("psum", [128, 512], "float32"),
    "pD": ("psum", [128, 512], "float32"),
    "pV": ("psum", [128, 512], "float32"),
    "pX": ("psum", [128, 512], "float32"),
    "pY": ("psum", [128, 512], "float32"),
    "pZ": ("psum", [128, 512], "float32"),
    "pK": ("psum", [128, 512], "float32"),
}
PSUM = [n for n in SCRATCH if SCRATCH[n][0] == "psum"]
SEMAPHORES = (["qv", "qs", "qp", "qg", "sent", "ld0", "ld1", "ld2", "ld3", "st0", "st1", "st2"]
              + ["l%d" % i for i in range(RO * NL)] + ["e%d" % i for i in range(RO * NL)])

ORDER = ("GA0a vGA0b K P0 MA0 U0 C0 GS0 GA1 mA0 E0 N0 P1 X0 MS0 mS0 F0 B0 "
         "MA1 U1 mA1 E1 C1 GS1 GA2 D1 N1 P2 X1 R0 MS1 mS1 F1 B1 "
         "MA2 U2 mA2 E2 C2 GS2 GA3 GS3a S X2 R1 MS2 mS2 F2 B2 vGS3b R2 "
         "MS3 F3 mS3 B3 MA3 x3 R3 mA3 y3 J0 J1 J2 J3 Z")


def rank_program(g, core, T, topo):
    rank = T.rank_of(core)
    if rank is None:
        return
    op = AluOpType
    copy_fn = ActivationFunctionType.Copy
    n_ranks = len(T.cores)
    Q = {"g": g, "v": g.vector, "s": g.scalar, "p": g.tensor, "y": g.sync}
    cnt = {"v": 0, "s": 0, "p": 0, "g": 0}
    known = {"g": {}, "v": {}, "s": {}, "p": {}, "y": {}}
    log = {}

    def need(q, outs, ins):
        evs = []
        for buf, lo, hi, w in [(o[1], o[2], o[3], True) for o in outs] + [(i[1], i[2], i[3], False) for i in ins]:
            for (lo2, hi2, w2, q2, s2, v2, c2) in log.get(buf, []):
                if q2 == q:
                    if not (w2 and (q != "p" or not w) and lo < hi2 and lo2 < hi):
                        continue
                elif buf in PSUM:
                    pass
                elif not ((w or w2) and lo < hi2 and lo2 < hi):
                    continue
                evs.append((s2, v2, c2))
        best = {}
        for s2, v2, c2 in evs:
            if known[q].get(s2, 0) < v2 and (s2 not in best or best[s2][0] < v2):
                best[s2] = (v2, c2)
        for s2 in list(best):
            if any(s3 != s2 and best[s3][1].get(s2, 0) >= best[s2][0] for s3 in best):
                continue
            v2, c2 = best[s2]
            Q[q].wait_ge(T.sem[s2], v2)
        for s2 in best:
            v2, c2 = best[s2]
            for s3 in c2:
                known[q][s3] = max(known[q].get(s3, 0), c2[s3])
            known[q][s2] = max(known[q].get(s2, 0), v2)

    def note(q, outs, ins, s, v, clock):
        for o in outs:
            log[o[1]] = [a for a in log.get(o[1], []) if not (o[2] <= a[0] and a[1] <= o[3])]
            log[o[1]].append((o[2], o[3], True, q, s, v, clock))
        for i in ins:
            log.setdefault(i[1], [])
            log[i[1]] = [a for a in log[i[1]] if a[2] or a[3] != q or not (i[2] <= a[0] and a[1] <= i[3])]
            log[i[1]].append((i[2], i[3], False, q, s, v, clock))

    def run(q, call, outs, ins):
        need(q, outs, ins)
        cnt[q] += 1
        call().then_inc(T.sem["q" + q], 1)
        clock = dict(known[q])
        clock["q" + q] = cnt[q]
        note(q, outs, ins, "q" + q, cnt[q], clock)

    def dma(q, out, in_, s):
        o = [out] if out[1] else []
        i = [in_] if in_[1] else []
        need(q, o, i)
        Q[q].dma_start(out[0], in_[0]).then_inc(T.sem[s], 16)
        note("dma", o, i, s, 16, dict(known[q]))

    def ext(ap):
        return (ap, None, 0, 0)

    def A(name, lo=0, hi=None, st=1):
        if hi is None:
            hi = SCRATCH[name][1][1]
        t = T[name]
        return (t[:, lo:hi] if st == 1 else t[:, lo:hi:st], name, lo, hi)

    def cp(out, in_):
        run("v", lambda: g.vector.tensor_copy(out[0], in_[0]), [out], [in_])

    def tt(out, a, b, o):
        run("v", lambda: g.vector.tensor_tensor(out[0], a[0], b[0], o), [out], [a, b])

    def ts(out, a, s1, s2, o1, o2=None):
        ins = [a] + [s for s in (s1, s2) if isinstance(s, tuple)]
        x1 = s1[0] if isinstance(s1, tuple) else s1
        x2 = s2[0] if isinstance(s2, tuple) else s2
        if o2 is None:
            run("v", lambda: g.vector.tensor_scalar(out[0], a[0], x1, None, o1), [out], ins)
        else:
            run("v", lambda: g.vector.tensor_scalar(out[0], a[0], x1, x2, o1, o2), [out], ins)

    def fill(out, c):
        run("v", lambda: g.vector.memset(out[0], c), [out], [])

    def scan(out, d0, d1, o0, o1):
        run("v", lambda: g.vector.tensor_tensor_scan(out[0], d0[0], d1[0], 0.0, o0, o1), [out], [d0, d1])

    def vgather(out, win, off):
        run("v", lambda: g.vector.tensor_copy(out[0], win[0].indirect(off[0])), [out], [win, off])

    def sgather(out, win, off):
        run("s", lambda: g.scalar.activation(out[0], win[0].indirect(off[0]), copy_fn), [out], [win, off])

    def scp(out, in_, scale=1.0, bias=0.0):
        ins = [in_] + ([scale] if isinstance(scale, tuple) else [])
        x = scale[0] if isinstance(scale, tuple) else scale
        run("s", lambda: g.scalar.activation(out[0], in_[0], copy_fn, bias=bias, scale=x), [out], ins)

    def mm(out, pairs, first=True, last=True):
        for n, (l, r) in enumerate(pairs):
            st, sp = first and n == 0, last and n == len(pairs) - 1
            run("p", lambda: g.tensor.matmul(out[0], l[0], r[0], st, sp), [out], [l, r])

    n_eng = min(len(topo.engines(a, b)) for a in T.cores for b in T.cores if a != b)
    sends = [0]

    def send(dst, out, in_, s):
        need("g", [], [in_])
        rid, pid, _ = topo.addr(dst)
        m = sum(1 << e for e in topo.engines(core, dst)[:n_eng])
        g.remote_dma(out[0], in_[0], T.sem[s], T.sem.sent, pid, rid, m)
        sends[0] += n_eng
        note("x", [out], [], s, n_eng, {})

    dma("y", A("nW", 0, 128), ext(T.ch[:, :]), "ld0")
    dma("s", A("wI"), ext(T.wt[:, :]), "ld1")
    dma("y", A("tab"), ext(T.xt[:, :]), "ld2")
    fill(A("slz"), 0)
    need("s", [("", "slz", 0, 1152)], [])
    g.scalar.dma_start(T.slz[0:128:16, :], T.sl[:, :]).then_inc(T.sem.ld3, 16)
    note("dma", [A("slz")], [], "ld3", 16, dict(known["s"]))
    run("g", lambda: g.iota(T.kp1[:, :], [[0, 8], [1, 16]], 1, 0, allow_small_or_imprecise_dtypes=True), [A("kp1")], [])
    run("g", lambda: g.iota(T.kI[:, 0:1], [[0, 1]], 0, 1), [A("kI", 0, 1)], [])
    run("g", lambda: g.affine_select(T.kp2[:, :], T.kp1[:, :], [[-16, 8], [0, 16]], op.is_ge, 0.0, 0, 1), [A("kp2")], [A("kp1")])
    run("g", lambda: g.affine_select(T.BK1[:, :], T.kp2[:, :], [[16, 8], [0, 16]], op.is_ge, 0.0, 15, -1), [A("BK1")], [A("kp2")])
    run("g", lambda: g.iota(T.cKi[:, :], [[4096, 4], [512, 8]], 0, 0), [A("cKi")], [])
    fill(A("mx"), 1.0)
    fill(A("mx", 0, 2048, 16), 0.0)
    cp(A("L", 0, 128), A("nW", 0, 128))

    def send_list(t, c):
        i = t * NL + c
        q = T.cores[(rank + 1 + t % (n_ranks - 1)) % n_ranks]
        send(q, A("Lr", i * 128, i * 128 + 128), A("L", i * 128, i * 128 + 128), "l%d" % i)

    def send_reply(t, c):
        i = t * NL + c
        p = T.cores[(rank - 1 - t % (n_ranks - 1)) % n_ranks]
        send(p, A("Eq", i * 8, i * 8 + 8), A("Er", i * 8, i * 8 + 8), "e%d" % i)

    send_list(0, 0)
    for n, m in ((0, 4032), (1, 63), (2, 31)):
        ts(A("wq", n, n + 1), A("wI"), m, None, op.bitwise_and)
    cp(A("wf", 0, 3), A("wq", 0, 3))
    cp(A("BKb"), A("BK1"))
    for k in range(16):
        ts(A("Bk", k * 128, k * 128 + 128), A("BKb"), k + 1.0, None, op.is_equal)
    scp(A("mn"), A("mx"), -512.0, 512.0)
    scp(A("Wk"), A("Bk"), A("wf", 2, 3))
    ts(A("Bp"), A("BK1"), 0.5, None, op.is_ge)
    ts(A("Bn"), A("BK1"), 0.5, -1.0, op.is_ge, op.mult)
    ts(A("Wh"), A("Bp"), A("wf", 0, 1), None, op.mult)
    ts(A("Wl"), A("Bp"), A("wf", 1, 2), None, op.mult)
    ts(A("kI", 1, 2), A("kI", 0, 1), 15, None, op.bitwise_and)
    ts(A("kf", 0, 1), A("kI", 1, 2), 64.0 * 613, -1048576.0, op.mult, op.add)
    ts(A("kf", 1, 2), A("kI", 1, 2), 32.0, None, op.mult)
    cp(A("kf", 2, 3), A("kf", 0, 1))
    ts(A("kf", 3, 4), A("kf", 0, 1), 64.0 * 77, None, op.add)
    ts(A("cK"), A("cKi"), A("kf", 1, 2), None, op.add)
    cp(A("slb"), A("slz"))
    for k in range(16):
        mm(A("pK", 0, 72), [(A("Bk", k * 128, k * 128 + 128), A("slb", k, 1152, 16))], k == 0, k == 15)
    ts(A("Bnk"), A("Bk"), -1.0, None, op.mult)
    fill(A("ones"), 1.0)

    def yv(c):
        return A("Y", c * 2048 + 15, c * 2048 + 2048, 16)

    def mv(c):
        return A("Mn", c * 2048 + 15, c * 2048 + 2048, 16)

    def sl(t, j):
        return A("slb", (t * 3 + j) * 128, (t * 3 + j) * 128 + 128)

    px3, pu3 = A("pZ", 0, 8), A("pZ", 32, 40)

    def half(x):
        return {"": (0, 128), "a": (0, 64), "b": (64, 128)}[x]

    def blk(name, k):
        return A(name, k * 128, k * 128 + 128)

    def piece(t, w):
        onv = w[0] == "v"
        w = w[1:] if onv else w
        kind = w.rstrip("0123ab")
        rest = w[len(kind):]
        c = int(rest[0]) if rest else 0
        lo, hi = half(rest[1:]) if rest else (0, 128)
        i = t * NL + c
        if kind in ("GA", "GS"):
            own = kind == "GA"
            out = A(("gA%d" if own else "gS%d") % (c % 2), lo * 16, hi * 16)
            (vgather if onv else sgather)(out, A("tab"), A("L" if own else "Lr", i * 128 + lo, i * 128 + hi))
        elif kind == "MA":
            scan(A("Y", c * 2048, c * 2048 + 2048), A("mx"), A("gA%d" % (c % 2)), op.mult, op.max)
        elif kind == "mA":
            scan(A("Mn", c * 2048, c * 2048 + 2048), A("mn"), A("gA%d" % (c % 2)), op.max, op.min)
        elif kind == "MS":
            scan(A("YS", lo * 16, hi * 16), A("mx", lo * 16, hi * 16), A("gS%d" % (c % 2), lo * 16, hi * 16), op.mult, op.max)
        elif kind == "mS":
            scan(A("MS", lo * 16, hi * 16), A("mn", lo * 16, hi * 16), A("gS%d" % (c % 2), lo * 16, hi * 16), op.max, op.min)
        elif kind == "U":
            mm(A("pU", 0, 128), [(A("Wh"), yv(c)), (A("Wl"), yv(c))])
        elif kind == "E":
            mm(A("pE", 0, 128), [(A("Bp"), yv(c)), (A("Bn"), mv(c))] + ([(A("Bp"), sl(t, 0))] if c == 0 else []))
        elif kind == "D":
            mm(A("pD", 0, 128), [(A("Bp"), yv(1)), (A("Bn"), mv(1)), (A("Bn"), yv(0)), (A("Bp"), mv(0))])
            mm(A("pD", 128, 256), [(A("Bp"), yv(0)), (A("Bn"), mv(0)), (A("Bp"), sl(t, 1))])
        elif kind == "N":
            if c == 0:
                cp(A("thr"), A("pE", 0, 128))
            else:
                tt(A("hd"), A("pD", 0, 128), A("h"), op.mult)
                tt(A("thr"), A("hd"), A("pD", 128, 256), op.add)
        elif kind == "S":
            for n in range(9 if t == 0 else 0):
                for d in (0, 8):
                    scp(A("a8", n * 16 + d, n * 16 + d + 8), A("pK", n * 8, n * 8 + 8))
        elif kind == "K":
            if t > 0:
                cp(A("nW", 0, 128), A("L", i * 128, i * 128 + 128))
                run("v", lambda: g.vector.tensor_reduce(T.cf[:, 32:33], T.pK[:, 80:88], AxisListType.X, op.add),
                    [A("cf", 32, 33)], [A("pK", 80, 88)])
                ts(A("ci", 32, 33), A("cf", 32, 33), -1.0, None, op.mult)
                ts(A("ci", 33, 34), A("ci", 32, 33), 31, None, op.bitwise_and)
                ts(A("kf", 2, 3), A("ci", 33, 34), 64.0, A("kf", 0, 1), op.mult, op.add)
                ts(A("kf", 3, 4), A("kf", 2, 3), 64.0 * 77, None, op.add)
        elif kind == "P":
            s = A("nW", c * 128, c * 128 + 128)
            if c == 0:
                ts(A("pV", 128, 256), s, 64.0, A("kf", 2, 3), op.mult, op.add)
            else:
                ts(A("pV", 128, 256), s, 64.0, 64.0 * 77, op.mult, op.add)
            cp(A("pV", 0, 128), s)
        elif kind == "C":
            cp(A("Ui"), A("pU", 0, 128))
            ts(A("ua"), A("Ui"), 4095, None, op.bitwise_and)
            tt(A("P"), A("ua"), A("pV", 0, 128), op.mult)
            p3 = A("P")
            if c > 0:
                ts(A("pV", 256, 384), A("P"), A("kf", 1 + c, 2 + c), None, op.add)
                tt(A("h"), A("pE", 0, 128), A("thr"), op.is_le)
                p3 = A("P3")
                tt(p3, A("pV", 256, 384), A("h"), op.mult)
            tt(A("Qi"), p3, A("pV", 128, 256), op.add)
            ts(A("nW", (c + 1) * 128, (c + 2) * 128), A("Qi"), 6, 4095, op.arith_shift_right, op.bitwise_and)
            cp(A("L", (i + 1) * 128, (i + 2) * 128), A("nW", (c + 1) * 128, (c + 2) * 128))
            send_list(t, c + 1)
        elif kind in ("X", "x", "y"):
            px = px3 if c == 3 else A("pX", 8 * c, 8 * c + 8)
            pu = pu3 if c == 3 else A("pX", 32 + 8 * c, 40 + 8 * c)
            ys = [A("Y", c * 2048 + 16 * k + 15, c * 2048 + 2048, 256) for k in range(16)]
            ms = [A("Mn", c * 2048 + 16 * k + 15, c * 2048 + 2048, 256) for k in range(16)]
            if kind != "y":
                mm(pu, [(blk("Wk", k), ys[k]) for k in range(16)])
                mm(px, [(blk("Bk", k), ys[k]) for k in range(16)], True, False)
            if kind != "x":
                mm(px, [(blk("Bnk", k), ms[k]) for k in range(16)], False, True)
        elif kind == "F":
            mm(A("pY", 8 * c, 8 * c + 8), [(blk("Bk", k), A("YS", 16 * k + 15, 2048, 256)) for k in range(16)], True, False)
        elif kind == "B":
            mm(A("pY", 8 * c, 8 * c + 8), [(blk("Bnk", k), A("MS", 16 * k + 15, 2048, 256)) for k in range(16)], False, True)
        elif kind in ("R", "r"):
            (cp if kind == "R" else scp)(A("Er", i * 8, i * 8 + 8), A("pY", 8 * c, 8 * c + 8))
            send_reply(t, c)
        elif kind == "J" and c < 2:
            for n in ([0, 1] if c == 0 else [2]):
                cp(A("cat", 16 * n, 16 * n + 8), A("pX", 8 * n, 8 * n + 8))
                tt(A("cat", 16 * n + 8, 16 * n + 16), A("pX", 8 * n, 8 * n + 8), A("Eq", (t * NL + n) * 8, (t * NL + n) * 8 + 8), op.add)
            st = A("cat", 0, 16) if c == 0 else A("cat", 48, 64)
            tt(A("dl", 0, 16), A("cat", 16 * c + 16, 16 * c + 32), st, op.subtract)
            j = t * 3 + c
            tt(A("HD", 16 * c, 16 * c + 16), A("dl", 0, 16), A("a8", j * 16, j * 16 + 16), op.is_le)
            for d in (0, 8):
                tt(A("dl", 16 + d, 24 + d), A("dl", d, d + 8), A("HD", 16 * c, 16 * c + 8), op.mult)
            tt(A("cat", 48 + 16 * c, 64 + 16 * c), st, A("dl", 16, 32), op.add)
            tt(A("rt", 8 * c, 8 * c + 8), A("HD", 16 * c, 16 * c + 8), A("HD", 16 * c + 8, 16 * c + 16), op.is_equal)
        elif kind == "J" and c == 2:
            cp(A("Ki", 0, 24), A("pX", 32, 56))
            ts(A("Ki", 32, 56), A("Ki", 0, 24), 31, None, op.bitwise_and)
            tt(A("K", 0, 24), A("Ki", 32, 56), A("cK", 0, 24), op.add)
            j = t * 3 + 2
            tt(A("cat", 80, 96), A("cat", 64, 80), A("a8", j * 16, j * 16 + 16), op.add)
            tt(A("rt", 16, 24), A("rt", 0, 8), A("rt", 8, 16), op.mult)
            tt(A("rt", 24, 32), A("rt", 0, 8), A("HD", 24, 32), op.mult)
            tt(A("cf", 0, 8), A("HD", 8, 16), A("K", 8, 16), op.mult)
            tt(A("cf", 8, 16), A("rt", 24, 32), A("K", 16, 24), op.mult)
            tt(A("cf", 16, 24), A("K", 0, 8), A("cf", 0, 8), op.max)
            tt(A("cf", 24, 32), A("cf", 16, 24), A("cf", 8, 16), op.max)
        elif kind == "J":
            cp(A("Ki", 24, 32), pu3)
            tt(A("rt", 32, 40), A("cat", 88, 96), px3, op.subtract)
            ts(A("Ki", 56, 64), A("Ki", 24, 32), 31, None, op.bitwise_and)
            tt(A("rt", 40, 48), px3, A("cat", 80, 88), op.is_le)
            tt(A("K", 24, 32), A("Ki", 56, 64), A("cK", 24, 32), op.add)
            tt(A("rt", 48, 56), A("rt", 16, 24), A("K", 24, 32), op.mult)
        elif kind == "Z":
            last = t == RO - 1
            n = (t * NL + 3) * 8
            tt(A("HD", 32, 40), A("Eq", n, n + 8), A("rt", 32, 40), op.is_le)
            tt(A("HD", 40, 48), A("HD", 32, 40), A("rt", 48, 56), op.mult)
            tt(A("ci", 0, 8), A("HD", 40, 48), A("cf", 24, 32), op.max)
            ts(A("ci", 8, 16), A("ci", 0, 8), 5, None, op.arith_shift_right)
            ts(A("ci", 16, 24), A("ci", 0, 8), 4095, None, op.bitwise_and)
            if last:
                cp(A("o3", 0, 4), A("ci", 16, 20))
                ts(A("o3", 4, 8), A("ci", 20, 24), -2048.0, None, op.add)
                sgather(A("old", 0, 64), A("tab", 0, 2048), A("o3", 0, 4))
                sgather(A("old", 64, 128), A("tab", 2048, 4096), A("o3", 4, 8))
                ts(A("o2"), A("ci", 8, 16), 16.0, 15.0, op.mult, op.add)
            else:
                cp(A("o1"), A("ci", 8, 16))
                cp(A("o3"), A("ci", 16, 24))
                sgather(A("old"), A("tab"), A("o3"))
                vgather(A("L", (i_next(t)) * 128, (i_next(t)) * 128 + 128), A("nW"), A("o1"))
                send_list(t + 1, 0)
                ts(A("o2"), A("ci", 8, 16), 16.0, 15.0, op.mult, op.add)
            parts = [(0, 64), (64, 128)] if last else [(0, 128)]
            for a, b in parts:
                yw, of = A("Y"), A("o2", a // 16, b // 16)
                run("v", lambda: g.vector.tensor_tensor(T.sm[:, a:b], yw[0].indirect(of[0]), T.old[:, a:b], op.add),
                    [A("sm", a, b)], [yw, of, A("old", a, b)])
                ts(A("sn", a, b), A("sm", a, b), 1, None, op.arith_shift_right)
                win, of3 = A("tab", 32 * a, 32 * b), A("o3", a // 16, b // 16)
                run("v", lambda: g.vector.tensor_copy(win[0].indirect(of3[0]), T.sn[:, a:b]), [win], [A("sn", a, b), of3])
                if last:
                    dma("y" if a == 0 else "s", ext(T.yx[:, 32 * a:32 * b]), win, "st0" if a == 0 else "st1")
            if last:
                cp(A("o1"), A("ci", 8, 16))
                vgather(A("fin"), A("nW"), A("o1"))
                dma("y", ext(T.yc[:, :]), A("fin"), "st2")
            else:
                tt(A("rt", 56, 64), A("HD", 32, 40), A("rt", 40, 48), op.is_equal)
                tt(A("r3"), A("rt", 56, 64), A("rt", 16, 24), op.mult)
                mm(A("pK", 80, 88), [(A("ones"), A("r3"))])

    def i_next(t):
        return (t + 1) * NL

    for t in range(RO):
        for w in ORDER.split():
            piece(t, w)

    for q in "vspg":
        g.wait_ge(T.sem["q" + q], cnt[q])
    g.wait_ge(T.sem.sent, sends[0])
    for s in ("ld0", "ld1", "ld2", "ld3", "st0", "st1", "st2"):
        g.wait_ge(T.sem[s], 16)
